import numpy as np, ml_dtypes
CORES = [4,132,140,148,156,164,172,180,188,196,204,212,220,228,236,244,252]
N = 17
def setup_inputs(rng):
    return {"x": rng.standard_normal((N, 128, 256), dtype=np.float32).astype(ml_dtypes.bfloat16)}
def reference(x):
    g = np.concatenate(list(x), axis=1)
    return {"y": np.broadcast_to(g, (N,) + g.shape)}

import comms_topo
from concourse.bass import DstId, RemoteDMATransfer

NQ = 9
BW = 256
RANK_CORE = 4
DIE1_SENDER = 0
XFWD = 3

DIE0_CALLS = [(0, [(1, 6), (2, 2), (3, 7), (4, 3)]), (1, [(5, 7)])]
DIE1_CALLS = [(1, [(8, 6), (7, 2), (6, 3)])]
EST = {1: 0, 2: 1, 3: 2, 4: 3, 5: 4, 8: 3, 7: 4, 6: 5}
GROUP = {1: 0, 2: 0, 3: 0, 4: 1, 8: 1, 5: 2, 6: 2, 7: 2}
NGROUPS = 3

SCRATCH = {
    "xs": ("dram", [128, BW], "bfloat16"),
    "slot": ("dram", [2, 128, BW], "bfloat16"),
    "land": ("sbuf", [128, 17 * BW], "bfloat16"),
}
SEMAPHORES = ["ld", "own", "inx", "in0", "in1", "g0", "g1", "g2", "sent", "stored"]


def chip_base(q, p):
    return p * 8 if q == 0 else 128 + (2 * (q - 1) + p) * 8


def place(core):
    h, c = core // 128, (core % 128) // 8
    if h == 0:
        return (0, c, core % 8) if c < 2 else None
    return (c // 2 + 1, c % 2, core % 8)


def has_rank(q, p):
    return not (q == 0 and p == 1)


def blk(q, p):
    return 0 if q == 0 else 2 * q - 1 + p


def slot_of():
    m = {}
    for slot, lst in DIE0_CALLS + DIE1_CALLS:
        for d, f in lst:
            m[d] = (slot, f)
    return m


def fwd_ops(q, p):
    ops = []
    own = chip_base(q, p) + RANK_CORE if has_rank(q, p) else None
    mate = chip_base(q, 1 - p) + RANK_CORE if has_rank(q, 1 - p) else None
    for d, (slot, f) in sorted(slot_of().items()):
        s = (q - d) % NQ
        if not has_rank(s, p):
            continue
        if own is not None and mate is not None:
            tg = [(mate, 0x00FF), (own, 0xFF00)]
        elif own is not None:
            tg = [(own, 0xFFFF)]
        else:
            tg = [(mate, 0x00FF)]
        ops.append((f, EST[d], slot, blk(s, p), GROUP[d], tg))
    if own is not None and mate is not None:
        ops.append((XFWD, -1, None, blk(q, p), 0, [(mate, 0x00FF)]))
    return ops


def bits(m):
    return bin(m).count("1")


def rank_program(g, core, T, topo):
    pl = place(core)
    if pl is None:
        return
    q, p, c = pl
    base = chip_base(q, p)

    def dst(d):
        rid, pid = topo.addr(d, core)
        return DstId(rid=rid, pnc=pid)

    def cols(b0, b1):
        return slice(b0 * BW, b1 * BW)

    def switch_transfer(slot, lst):
        dsts = [chip_base((q + d) % NQ, p) + f for d, f in lst]
        return RemoteDMATransfer(dst_ids=[dst(x) for x in dsts], dma_engine_mask=0x00FF, remote_sem=T.sem["in%d" % slot],
                                 srcs=[T.xs[:]], dsts=[T.slot[slot] for x in dsts])

    sent = 0
    if c == RANK_CORE and has_rank(q, p):
        me = blk(q, p)
        g.sync.dma_start(T.xs[:], T.x[:]).then_inc(T.sem.ld, 16)
        g.scalar.dma_start(T.land[:, cols(me, me + 1)], T.x[:]).then_inc(T.sem.own, 16)
        g.wait_ge(T.sem.ld, 16)
        onchip = [base + DIE1_SENDER] + ([base + XFWD] if has_rank(q, 1 - p) else [])
        for i, (slot, lst) in enumerate(DIE0_CALLS):
            tr = [switch_transfer(slot, lst)]
            sent += 8
            if i == 0:
                tr.append(RemoteDMATransfer(dst_ids=[dst(x) for x in onchip], dma_engine_mask=0xFF00, remote_sem=T.sem.inx,
                                            srcs=[T.xs[:]], dsts=[T.xs[:] for x in onchip]))
                sent += 8
            g.remote_dma_fused(tr, local_sem=T.sem.sent)
        need = [0] * NGROUPS
        blocks = [[] for i in range(NGROUPS)]
        blocks[0].append(me)
        for pp in (p, 1 - p):
            for f, o, slot, b, grp, tg in fwd_ops(q, pp):
                for dcore, m in tg:
                    if dcore == core:
                        need[grp] += bits(m)
                        blocks[grp].append(b)
        queues = [g.sync, g.scalar]
        waited = [set(), set()]
        n = 0
        for grp in range(NGROUPS):
            bs = sorted(blocks[grp])
            runs = []
            for b in bs:
                if runs and runs[-1][1] == b:
                    runs[-1][1] = b + 1
                else:
                    runs.append([b, b + 1])
            for b0, b1 in runs:
                k = n % 2
                if grp not in waited[k]:
                    waited[k].add(grp)
                    if grp == 0:
                        queues[k].wait_ge(T.sem.own, 16)
                    queues[k].wait_ge(T.sem["g%d" % grp], need[grp])
                queues[k].dma_start(T.y[:, cols(b0, b1)], T.land[:, cols(b0, b1)]).then_inc(T.sem.stored, 16)
                n += 1
        g.wait_ge(T.sem.sent, sent)
        g.wait_ge(T.sem.stored, 16 * n)
        return

    if c == DIE1_SENDER and has_rank(q, p):
        g.wait_ge(T.sem.inx, 8)
        for slot, lst in DIE1_CALLS:
            g.remote_dma_fused([switch_transfer(slot, lst)], local_sem=T.sem.sent)
            sent += 8
        g.wait_ge(T.sem.sent, sent)
        return

    mine = sorted([o for o in fwd_ops(q, p) if o[0] == c], key=lambda o: o[1])
    for f, o, slot, b, grp, tg in mine:
        if slot is None:
            g.wait_ge(T.sem.inx, 8)
            src = T.xs[:]
        else:
            g.wait_ge(T.sem["in%d" % slot], 8)
            src = T.slot[slot]
        tr = [RemoteDMATransfer(dst_ids=[dst(dcore)], dma_engine_mask=m, remote_sem=T.sem["g%d" % grp],
                                srcs=[src], dsts=[T.land[:, cols(b, b + 1)]]) for dcore, m in tg]
        g.remote_dma_fused(tr, local_sem=T.sem.sent)
        sent += sum(bits(m) for dcore, m in tg)
    if sent:
        g.wait_ge(T.sem.sent, sent)
